import numpy as np
import ml_dtypes

BF16 = ml_dtypes.bfloat16


def bf(x):
    return np.asarray(x, np.float32).astype(BF16)


def f32(x):
    return np.asarray(x, np.float32)


def f64(x):
    return np.asarray(x).astype(np.float64)


def striped(idx):
    return np.tile(idx.reshape(-1, 16).T, (8, 1))


S, K, M, N, E, Q = 256, 256, 256, 512, 4, 128


def two_experts():
    first = np.random.permutation(S).reshape(E, S // E)
    return np.concatenate([np.random.permutation(np.concatenate([first[e], first[(e + 1) % E]])) for e in range(E)])


def setup_inputs():
    return {"table": bf(np.random.standard_normal((S, K))), "w": bf(np.random.standard_normal((E, K, M)) / np.sqrt(K)), "b": f32(0.5 * np.random.standard_normal((M, 1))), "offs": striped(two_experts())}


def reference(table, w, b, offs):
    idx = offs[:16].T.reshape(-1)
    x = f64(table)[idx].T
    y = np.concatenate([f64(w)[e].T @ x[:, e * Q : (e + 1) * Q] for e in range(E)], axis=1)
    return np.maximum(y + f64(b), 0.0)

@@ -1,0 +1,78 @@
+import concourse.mybir as mybir
+from concourse.masks import make_identity
+
+BF16, F32, U16 = mybir.dt.bfloat16, mybir.dt.float32, mybir.dt.uint16
+
+P = 128
+S, K, M, N, E = 256, 256, 256, 512, 4
+Q = N // E
+TOKEN_BLOCKS, K_BLOCKS, M_BLOCKS = S // P, K // P, M // P
+Q_COLS = Q // 16
+
+FLOPS = 2 * K * M * N
+
+
+def tile_gather_matmul_kernel(tc, table, w, b, offs, out):
+    nc = tc.nc
+    with (
+        tc.tile_pool(name="held", bufs=1) as held,
+        tc.psum_pool(name="flip", bufs=1) as flip,
+        tc.psum_pool(name="sums", bufs=1) as sums,
+    ):
+        offsets = held.tile([P, N // 16], U16, name="offsets")
+        nc.sync.dma_start(offsets[:], offs)
+
+        token_rows = held.tile([P, TOKEN_BLOCKS, K], BF16, name="token_rows")
+        nc.scalar.dma_start(token_rows[:], table.rearrange("(t p) k -> p t k", p=P))
+
+        w_view = w.rearrange("e (c p) m -> e p c m", p=P)
+        weights = [held.tile([P, K_BLOCKS, M], BF16, name=f"weights{e}") for e in range(E)]
+        for e in range(E):
+            queue = nc.sync if e % 2 == 0 else nc.scalar
+            queue.dma_start(weights[e][:], w_view[e])
+
+        bias = held.tile([P, M_BLOCKS], F32, name="bias")
+        with nc.allow_non_contiguous_dma(reason="one float32 to a partition and block"):
+            nc.sync.dma_start(bias[:], b.rearrange("(a p) o -> p (a o)", p=P))
+
+        identity = held.tile([P, P], BF16, name="identity")
+        make_identity(nc, identity[:])
+
+        features = [held.tile([P, S], BF16, name=f"features{c}") for c in range(K_BLOCKS)]
+        for c in range(K_BLOCKS):
+            flipped = flip.tile([P, S], BF16, name=f"flipped{c}")
+            for t in range(TOKEN_BLOCKS):
+                nc.tensor.transpose(
+                    flipped[:, t * P : (t + 1) * P],
+                    token_rows[:, t, c * P : (c + 1) * P],
+                    identity[:],
+                )
+            if c % 2 == 0:
+                nc.vector.tensor_copy(features[c][:], flipped[:])
+            else:
+                nc.scalar.copy(features[c][:], flipped[:])
+
+        for a in range(M_BLOCKS):
+            bank = sums.tile([P, N], F32, name=f"bank{a}")
+            for e in range(E):
+                picked = offsets[:, e * Q_COLS : (e + 1) * Q_COLS]
+                for c in range(K_BLOCKS):
+                    nc.tensor.matmul(
+                        bank[:, e * Q : (e + 1) * Q],
+                        weights[e][:, c, a * P : (a + 1) * P],
+                        features[c][:].indirect(picked),
+                        start=(c == 0),
+                        stop=(c == K_BLOCKS - 1),
+                    )
+            result = held.tile([P, N], F32, name=f"result{a}")
+            if a % 2 == 0:
+                nc.vector.tensor_scalar(
+                    result[:], bank[:], bias[:, a : a + 1], 0.0,
+                    op0=mybir.AluOpType.add, op1=mybir.AluOpType.max,
+                )
+                nc.sync.dma_start(out[a * P : (a + 1) * P, :], result[:])
+            else:
+                nc.scalar.activation(
+                    result[:], bank[:], mybir.ActivationFunctionType.Relu, bias=bias[:, a : a + 1]
+                )
+                nc.scalar.dma_start(out[a * P : (a + 1) * P, :], result[:])

@@ -17,7 +17,7 @@ def tile_gather_matmul_kernel(tc, table, w, b, offs, out):
     with (
         tc.tile_pool(name="held", bufs=1) as held,
         tc.psum_pool(name="flip", bufs=1) as flip,
-        tc.psum_pool(name="sums", bufs=1) as sums,
+        tc.psum_pool(name="sums", bufs=2) as sums,
     ):
         offsets = held.tile([P, N // 16], U16, name="offsets")
         nc.sync.dma_start(offsets[:], offs)
@@ -40,39 +40,34 @@ def tile_gather_matmul_kernel(tc, table, w, b, offs, out):
 
         features = [held.tile([P, S], BF16, name=f"features{c}") for c in range(K_BLOCKS)]
         for c in range(K_BLOCKS):
-            flipped = flip.tile([P, S], BF16, name=f"flipped{c}")
             for t in range(TOKEN_BLOCKS):
-                nc.tensor.transpose(
-                    flipped[:, t * P : (t + 1) * P],
-                    token_rows[:, t, c * P : (c + 1) * P],
-                    identity[:],
-                )
-            if c % 2 == 0:
-                nc.vector.tensor_copy(features[c][:], flipped[:])
-            else:
-                nc.scalar.copy(features[c][:], flipped[:])
+                flipped = flip.tile([P, P], BF16, name=f"flipped{c}{t}")
+                nc.tensor.transpose(flipped[:], token_rows[:, t, c * P : (c + 1) * P], identity[:])
+                if c % 2 == 0:
+                    nc.vector.tensor_copy(features[c][:, t * P : (t + 1) * P], flipped[:])
+                else:
+                    nc.scalar.copy(features[c][:, t * P : (t + 1) * P], flipped[:])
 
-        for a in range(M_BLOCKS):
-            bank = sums.tile([P, N], F32, name=f"bank{a}")
-            for e in range(E):
-                picked = offsets[:, e * Q_COLS : (e + 1) * Q_COLS]
-                for c in range(K_BLOCKS):
+        result = [held.tile([P, N], F32, name=f"result{a}") for a in range(M_BLOCKS)]
+        for e in range(E):
+            picked = offsets[:, e * Q_COLS : (e + 1) * Q_COLS]
+            columns = slice(e * Q, (e + 1) * Q)
+            banks = [sums.tile([P, Q], F32, name=f"bank{a}") for a in range(M_BLOCKS)]
+            for c in range(K_BLOCKS):
+                for a in range(M_BLOCKS):
                     nc.tensor.matmul(
-                        bank[:, e * Q : (e + 1) * Q],
+                        banks[a][:],
                         weights[e][:, c, a * P : (a + 1) * P],
                         features[c][:].indirect(picked),
                         start=(c == 0),
                         stop=(c == K_BLOCKS - 1),
                     )
-            result = held.tile([P, N], F32, name=f"result{a}")
-            if a % 2 == 0:
-                nc.vector.tensor_scalar(
-                    result[:], bank[:], bias[:, a : a + 1], 0.0,
-                    op0=mybir.AluOpType.add, op1=mybir.AluOpType.max,
-                )
-                nc.sync.dma_start(out[a * P : (a + 1) * P, :], result[:])
-            else:
-                nc.scalar.activation(
-                    result[:], bank[:], mybir.ActivationFunctionType.Relu, bias=bias[:, a : a + 1]
-                )
-                nc.scalar.dma_start(out[a * P : (a + 1) * P, :], result[:])
+            nc.vector.tensor_scalar(
+                result[0][:, columns], banks[0][:], bias[:, 0:1], 0.0,
+                op0=mybir.AluOpType.add, op1=mybir.AluOpType.max,
+            )
+            nc.sync.dma_start(out[0:P, columns], result[0][:, columns])
+            nc.scalar.activation(
+                result[1][:, columns], banks[1][:], mybir.ActivationFunctionType.Relu, bias=bias[:, 1:2]
+            )
+            nc.scalar.dma_start(out[P : 2 * P, columns], result[1][:, columns])

@@ -9,6 +9,10 @@ Q = N // E
 TOKEN_BLOCKS, K_BLOCKS, M_BLOCKS = S // P, K // P, M // P
 Q_COLS = Q // 16
 
+WARM_COLS = 512
+WARM_BEFORE_TABLE = 4
+WARM_BEFORE_SUMS = 2
+
 FLOPS = 2 * K * M * N
 
 
@@ -16,7 +20,7 @@ def tile_gather_matmul_kernel(tc, table, w, b, offs, out):
     nc = tc.nc
     with (
         tc.tile_pool(name="held", bufs=1) as held,
-        tc.psum_pool(name="flip", bufs=1) as flip,
+        tc.psum_pool(name="flip", bufs=4) as flip,
         tc.psum_pool(name="sums", bufs=2) as sums,
     ):
         offsets = held.tile([P, N // 16], U16, name="offsets")
@@ -35,18 +39,30 @@ def tile_gather_matmul_kernel(tc, table, w, b, offs, out):
         with nc.allow_non_contiguous_dma(reason="one float32 to a partition and block"):
             nc.sync.dma_start(bias[:], b.rearrange("(a p) o -> p (a o)", p=P))
 
+        zeros = held.tile([P, WARM_COLS], BF16, name="zeros")
+        nc.vector.memset(zeros[:], 0.0)
+
+        def idle_matmuls(count):
+            unused = flip.tile([P, WARM_COLS], F32, name="unused", tag="flipped")
+            for i in range(count):
+                nc.tensor.matmul(unused[:], zeros[:, 0:P], zeros[:], start=True, stop=True)
+
+        idle_matmuls(WARM_BEFORE_TABLE)
+
         identity = held.tile([P, P], BF16, name="identity")
         make_identity(nc, identity[:])
 
         features = [held.tile([P, S], BF16, name=f"features{c}") for c in range(K_BLOCKS)]
         for c in range(K_BLOCKS):
             for t in range(TOKEN_BLOCKS):
-                flipped = flip.tile([P, P], BF16, name=f"flipped{c}{t}")
+                flipped = flip.tile([P, P], BF16, name="flipped")
                 nc.tensor.transpose(flipped[:], token_rows[:, t, c * P : (c + 1) * P], identity[:])
                 if c % 2 == 0:
                     nc.vector.tensor_copy(features[c][:, t * P : (t + 1) * P], flipped[:])
                 else:
                     nc.scalar.copy(features[c][:, t * P : (t + 1) * P], flipped[:])
+
+        idle_matmuls(WARM_BEFORE_SUMS)
 
         result = [held.tile([P, N], F32, name=f"result{a}") for a in range(M_BLOCKS)]
         for e in range(E):

@@ -9,10 +9,6 @@ Q = N // E
 TOKEN_BLOCKS, K_BLOCKS, M_BLOCKS = S // P, K // P, M // P
 Q_COLS = Q // 16
 
-WARM_COLS = 512
-WARM_BEFORE_TABLE = 4
-WARM_BEFORE_SUMS = 2
-
 FLOPS = 2 * K * M * N
 
 
@@ -20,14 +16,20 @@ def tile_gather_matmul_kernel(tc, table, w, b, offs, out):
     nc = tc.nc
     with (
         tc.tile_pool(name="held", bufs=1) as held,
-        tc.psum_pool(name="flip", bufs=4) as flip,
+        tc.psum_pool(name="flip", bufs=1) as flip,
         tc.psum_pool(name="sums", bufs=2) as sums,
     ):
         offsets = held.tile([P, N // 16], U16, name="offsets")
         nc.sync.dma_start(offsets[:], offs)
 
-        token_rows = held.tile([P, TOKEN_BLOCKS, K], BF16, name="token_rows")
-        nc.scalar.dma_start(token_rows[:], table.rearrange("(t p) k -> p t k", p=P))
+        token_rows = [held.tile([P, K], BF16, name=f"token_rows{t}") for t in range(TOKEN_BLOCKS)]
+        for t in range(TOKEN_BLOCKS):
+            queue = nc.sync if t % 2 == 0 else nc.scalar
+            queue.dma_start(token_rows[t][:], table[t * P : (t + 1) * P, :])
+
+        bias = held.tile([P, M_BLOCKS], F32, name="bias")
+        with nc.allow_non_contiguous_dma(reason="one float32 to a partition and block"):
+            nc.scalar.dma_start(bias[:], b.rearrange("(a p) o -> p (a o)", p=P))
 
         w_view = w.rearrange("e (c p) m -> e p c m", p=P)
         weights = [held.tile([P, K_BLOCKS, M], BF16, name=f"weights{e}") for e in range(E)]
@@ -35,34 +37,18 @@ def tile_gather_matmul_kernel(tc, table, w, b, offs, out):
             queue = nc.sync if e % 2 == 0 else nc.scalar
             queue.dma_start(weights[e][:], w_view[e])
 
-        bias = held.tile([P, M_BLOCKS], F32, name="bias")
-        with nc.allow_non_contiguous_dma(reason="one float32 to a partition and block"):
-            nc.sync.dma_start(bias[:], b.rearrange("(a p) o -> p (a o)", p=P))
-
-        zeros = held.tile([P, WARM_COLS], BF16, name="zeros")
-        nc.vector.memset(zeros[:], 0.0)
-
-        def idle_matmuls(count):
-            unused = flip.tile([P, WARM_COLS], F32, name="unused", tag="flipped")
-            for i in range(count):
-                nc.tensor.matmul(unused[:], zeros[:, 0:P], zeros[:], start=True, stop=True)
-
-        idle_matmuls(WARM_BEFORE_TABLE)
-
         identity = held.tile([P, P], BF16, name="identity")
         make_identity(nc, identity[:])
 
         features = [held.tile([P, S], BF16, name=f"features{c}") for c in range(K_BLOCKS)]
         for c in range(K_BLOCKS):
             for t in range(TOKEN_BLOCKS):
-                flipped = flip.tile([P, P], BF16, name="flipped")
-                nc.tensor.transpose(flipped[:], token_rows[:, t, c * P : (c + 1) * P], identity[:])
+                flipped = flip.tile([P, P], BF16, name=f"flipped{c}{t}")
+                nc.tensor.transpose(flipped[:], token_rows[t][:, c * P : (c + 1) * P], identity[:])
                 if c % 2 == 0:
                     nc.vector.tensor_copy(features[c][:, t * P : (t + 1) * P], flipped[:])
                 else:
                     nc.scalar.copy(features[c][:, t * P : (t + 1) * P], flipped[:])
-
-        idle_matmuls(WARM_BEFORE_SUMS)
 
         result = [held.tile([P, N], F32, name=f"result{a}") for a in range(M_BLOCKS)]
         for e in range(E):

@@ -19,13 +19,12 @@ def tile_gather_matmul_kernel(tc, table, w, b, offs, out):
         tc.psum_pool(name="flip", bufs=1) as flip,
         tc.psum_pool(name="sums", bufs=2) as sums,
     ):
+        token_rows = [held.tile([P, K], BF16, name=f"token_rows{t}") for t in range(TOKEN_BLOCKS)]
+        nc.sync.dma_start(token_rows[0][:], table[0:P, :])
+        nc.scalar.dma_start(token_rows[1][:], table[P : 2 * P, :])
+
         offsets = held.tile([P, N // 16], U16, name="offsets")
         nc.sync.dma_start(offsets[:], offs)
-
-        token_rows = [held.tile([P, K], BF16, name=f"token_rows{t}") for t in range(TOKEN_BLOCKS)]
-        for t in range(TOKEN_BLOCKS):
-            queue = nc.sync if t % 2 == 0 else nc.scalar
-            queue.dma_start(token_rows[t][:], table[t * P : (t + 1) * P, :])
 
         bias = held.tile([P, M_BLOCKS], F32, name="bias")
         with nc.allow_non_contiguous_dma(reason="one float32 to a partition and block"):
@@ -34,8 +33,7 @@ def tile_gather_matmul_kernel(tc, table, w, b, offs, out):
         w_view = w.rearrange("e (c p) m -> e p c m", p=P)
         weights = [held.tile([P, K_BLOCKS, M], BF16, name=f"weights{e}") for e in range(E)]
         for e in range(E):
-            queue = nc.sync if e % 2 == 0 else nc.scalar
-            queue.dma_start(weights[e][:], w_view[e])
+            nc.sync.dma_start(weights[e][:], w_view[e])
 
         identity = held.tile([P, P], BF16, name="identity")
         make_identity(nc, identity[:])

@@ -43,10 +43,7 @@ def tile_gather_matmul_kernel(tc, table, w, b, offs, out):
             for t in range(TOKEN_BLOCKS):
                 flipped = flip.tile([P, P], BF16, name=f"flipped{c}{t}")
                 nc.tensor.transpose(flipped[:], token_rows[t][:, c * P : (c + 1) * P], identity[:])
-                if c % 2 == 0:
-                    nc.vector.tensor_copy(features[c][:, t * P : (t + 1) * P], flipped[:])
-                else:
-                    nc.scalar.copy(features[c][:, t * P : (t + 1) * P], flipped[:])
+                nc.vector.tensor_copy(features[c][:, t * P : (t + 1) * P], flipped[:])
 
         result = [held.tile([P, N], F32, name=f"result{a}") for a in range(M_BLOCKS)]
         for e in range(E):
@@ -62,12 +59,9 @@ def tile_gather_matmul_kernel(tc, table, w, b, offs, out):
                         start=(c == 0),
                         stop=(c == K_BLOCKS - 1),
                     )
-            nc.vector.tensor_scalar(
-                result[0][:, columns], banks[0][:], bias[:, 0:1], 0.0,
-                op0=mybir.AluOpType.add, op1=mybir.AluOpType.max,
-            )
-            nc.sync.dma_start(out[0:P, columns], result[0][:, columns])
-            nc.scalar.activation(
-                result[1][:, columns], banks[1][:], mybir.ActivationFunctionType.Relu, bias=bias[:, 1:2]
-            )
-            nc.scalar.dma_start(out[P : 2 * P, columns], result[1][:, columns])
+            for a, queue in enumerate((nc.sync, nc.scalar)):
+                nc.vector.tensor_scalar(
+                    result[a][:, columns], banks[a][:], bias[:, a : a + 1], 0.0,
+                    op0=mybir.AluOpType.add, op1=mybir.AluOpType.max,
+                )
+                queue.dma_start(out[a * P : (a + 1) * P, columns], result[a][:, columns])

@@ -8,6 +8,8 @@ S, K, M, N, E = 256, 256, 256, 512, 4
 Q = N // E
 TOKEN_BLOCKS, K_BLOCKS, M_BLOCKS = S // P, K // P, M // P
 Q_COLS = Q // 16
+WARM_COLUMNS = 512
+WARM_MATMULS = 3
 
 FLOPS = 2 * K * M * N
 
@@ -16,7 +18,7 @@ def tile_gather_matmul_kernel(tc, table, w, b, offs, out):
     nc = tc.nc
     with (
         tc.tile_pool(name="held", bufs=1) as held,
-        tc.psum_pool(name="flip", bufs=1) as flip,
+        tc.psum_pool(name="flip", bufs=4) as flip,
         tc.psum_pool(name="sums", bufs=2) as sums,
     ):
         token_rows = [held.tile([P, K], BF16, name=f"token_rows{t}") for t in range(TOKEN_BLOCKS)]
@@ -35,13 +37,19 @@ def tile_gather_matmul_kernel(tc, table, w, b, offs, out):
         for e in range(E):
             nc.sync.dma_start(weights[e][:], w_view[e])
 
+        ones = held.tile([P, WARM_COLUMNS], BF16, name="ones")
+        nc.vector.memset(ones[:], 1.0)
+        unread = flip.tile([P, WARM_COLUMNS], F32, name="unread", tag="flip")
+        for repeat in range(WARM_MATMULS):
+            nc.tensor.matmul(unread[:], ones[:, 0:P], ones[:], start=True, stop=True)
+
         identity = held.tile([P, P], BF16, name="identity")
         make_identity(nc, identity[:])
 
         features = [held.tile([P, S], BF16, name=f"features{c}") for c in range(K_BLOCKS)]
         for c in range(K_BLOCKS):
             for t in range(TOKEN_BLOCKS):
-                flipped = flip.tile([P, P], BF16, name=f"flipped{c}{t}")
+                flipped = flip.tile([P, P], BF16, name=f"flipped{c}{t}", tag="flip")
                 nc.tensor.transpose(flipped[:], token_rows[t][:, c * P : (c + 1) * P], identity[:])
                 nc.vector.tensor_copy(features[c][:, t * P : (t + 1) * P], flipped[:])
 

@@ -8,8 +8,7 @@ S, K, M, N, E = 256, 256, 256, 512, 4
 Q = N // E
 TOKEN_BLOCKS, K_BLOCKS, M_BLOCKS = S // P, K // P, M // P
 Q_COLS = Q // 16
-WARM_COLUMNS = 512
-WARM_MATMULS = 3
+WARM_MATMULS = 12
 
 FLOPS = 2 * K * M * N
 
@@ -37,11 +36,11 @@ def tile_gather_matmul_kernel(tc, table, w, b, offs, out):
         for e in range(E):
             nc.sync.dma_start(weights[e][:], w_view[e])
 
-        ones = held.tile([P, WARM_COLUMNS], BF16, name="ones")
+        ones = held.tile([P, P], BF16, name="ones")
         nc.vector.memset(ones[:], 1.0)
-        unread = flip.tile([P, WARM_COLUMNS], F32, name="unread", tag="flip")
+        unread = flip.tile([P, P], F32, name="unread", tag="flip")
         for repeat in range(WARM_MATMULS):
-            nc.tensor.matmul(unread[:], ones[:, 0:P], ones[:], start=True, stop=True)
+            nc.tensor.matmul(unread[:], ones[:], ones[:], start=True, stop=True)
 
         identity = held.tile([P, P], BF16, name="identity")
         make_identity(nc, identity[:])

@@ -8,6 +8,7 @@ S, K, M, N, E = 256, 256, 256, 512, 4
 Q = N // E
 TOKEN_BLOCKS, K_BLOCKS, M_BLOCKS = S // P, K // P, M // P
 Q_COLS = Q // 16
+PSUM_BANKS = 8
 WARM_MATMULS = 12
 
 FLOPS = 2 * K * M * N
@@ -17,8 +18,7 @@ def tile_gather_matmul_kernel(tc, table, w, b, offs, out):
     nc = tc.nc
     with (
         tc.tile_pool(name="held", bufs=1) as held,
-        tc.psum_pool(name="flip", bufs=4) as flip,
-        tc.psum_pool(name="sums", bufs=2) as sums,
+        tc.psum_pool(name="psum", bufs=PSUM_BANKS) as psum,
     ):
         token_rows = [held.tile([P, K], BF16, name=f"token_rows{t}") for t in range(TOKEN_BLOCKS)]
         nc.sync.dma_start(token_rows[0][:], table[0:P, :])
@@ -38,7 +38,7 @@ def tile_gather_matmul_kernel(tc, table, w, b, offs, out):
 
         ones = held.tile([P, P], BF16, name="ones")
         nc.vector.memset(ones[:], 1.0)
-        unread = flip.tile([P, P], F32, name="unread", tag="flip")
+        unread = psum.tile([P, P], F32, name="unread", tag="bank")
         for repeat in range(WARM_MATMULS):
             nc.tensor.matmul(unread[:], ones[:], ones[:], start=True, stop=True)
 
@@ -48,7 +48,7 @@ def tile_gather_matmul_kernel(tc, table, w, b, offs, out):
         features = [held.tile([P, S], BF16, name=f"features{c}") for c in range(K_BLOCKS)]
         for c in range(K_BLOCKS):
             for t in range(TOKEN_BLOCKS):
-                flipped = flip.tile([P, P], BF16, name=f"flipped{c}{t}", tag="flip")
+                flipped = psum.tile([P, P], BF16, name=f"flipped{c}{t}", tag="bank")
                 nc.tensor.transpose(flipped[:], token_rows[t][:, c * P : (c + 1) * P], identity[:])
                 nc.vector.tensor_copy(features[c][:, t * P : (t + 1) * P], flipped[:])
 
@@ -56,7 +56,7 @@ def tile_gather_matmul_kernel(tc, table, w, b, offs, out):
         for e in range(E):
             picked = offsets[:, e * Q_COLS : (e + 1) * Q_COLS]
             columns = slice(e * Q, (e + 1) * Q)
-            banks = [sums.tile([P, Q], F32, name=f"bank{a}") for a in range(M_BLOCKS)]
+            banks = [psum.tile([P, Q], F32, name=f"sums{e}{a}", tag="bank") for a in range(M_BLOCKS)]
             for c in range(K_BLOCKS):
                 for a in range(M_BLOCKS):
                     nc.tensor.matmul(

@@ -28,8 +28,7 @@ def tile_gather_matmul_kernel(tc, table, w, b, offs, out):
         nc.sync.dma_start(offsets[:], offs)
 
         bias = held.tile([P, M_BLOCKS], F32, name="bias")
-        with nc.allow_non_contiguous_dma(reason="one float32 to a partition and block"):
-            nc.scalar.dma_start(bias[:], b.rearrange("(a p) o -> p (a o)", p=P))
+        nc.scalar.dma_start(bias[:], b.rearrange("(p a) o -> p (a o)", a=M_BLOCKS))
 
         w_view = w.rearrange("e (c p) m -> e p c m", p=P)
         weights = [held.tile([P, K_BLOCKS, M], BF16, name=f"weights{e}") for e in range(E)]
@@ -52,6 +51,7 @@ def tile_gather_matmul_kernel(tc, table, w, b, offs, out):
                 nc.tensor.transpose(flipped[:], token_rows[t][:, c * P : (c + 1) * P], identity[:])
                 nc.vector.tensor_copy(features[c][:, t * P : (t + 1) * P], flipped[:])
 
+        out_view = out.rearrange("(p a) n -> a p n", a=M_BLOCKS)
         result = [held.tile([P, N], F32, name=f"result{a}") for a in range(M_BLOCKS)]
         for e in range(E):
             picked = offsets[:, e * Q_COLS : (e + 1) * Q_COLS]
@@ -61,7 +61,7 @@ def tile_gather_matmul_kernel(tc, table, w, b, offs, out):
                 for a in range(M_BLOCKS):
                     nc.tensor.matmul(
                         banks[a][:],
-                        weights[e][:, c, a * P : (a + 1) * P],
+                        weights[e][:, c, a::M_BLOCKS],
                         features[c][:].indirect(picked),
                         start=(c == 0),
                         stop=(c == K_BLOCKS - 1),
@@ -71,4 +71,4 @@ def tile_gather_matmul_kernel(tc, table, w, b, offs, out):
                     result[a][:, columns], banks[a][:], bias[:, a : a + 1], 0.0,
                     op0=mybir.AluOpType.add, op1=mybir.AluOpType.max,
                 )
-                queue.dma_start(out[a * P : (a + 1) * P, columns], result[a][:, columns])
+                queue.dma_start(out_view[a][:, columns], result[a][:, columns])

@@ -30,7 +30,7 @@ def tile_gather_matmul_kernel(tc, table, w, b, offs, out):
         bias = held.tile([P, M_BLOCKS], F32, name="bias")
         nc.scalar.dma_start(bias[:], b.rearrange("(p a) o -> p (a o)", a=M_BLOCKS))
 
-        w_view = w.rearrange("e (c p) m -> e p c m", p=P)
+        w_view = w.rearrange("e (p c) m -> e p c m", c=K_BLOCKS)
         weights = [held.tile([P, K_BLOCKS, M], BF16, name=f"weights{e}") for e in range(E)]
         for e in range(E):
             nc.sync.dma_start(weights[e][:], w_view[e])
@@ -48,7 +48,7 @@ def tile_gather_matmul_kernel(tc, table, w, b, offs, out):
         for c in range(K_BLOCKS):
             for t in range(TOKEN_BLOCKS):
                 flipped = psum.tile([P, P], BF16, name=f"flipped{c}{t}", tag="bank")
-                nc.tensor.transpose(flipped[:], token_rows[t][:, c * P : (c + 1) * P], identity[:])
+                nc.tensor.transpose(flipped[:], token_rows[t][:, c::K_BLOCKS], identity[:])
                 nc.vector.tensor_copy(features[c][:, t * P : (t + 1) * P], flipped[:])
 
         out_view = out.rearrange("(p a) n -> a p n", a=M_BLOCKS)

@@ -41,6 +41,9 @@ def tile_gather_matmul_kernel(tc, table, w, b, offs, out):
         for repeat in range(WARM_MATMULS):
             nc.tensor.matmul(unread[:], ones[:], ones[:], start=True, stop=True)
 
+        relu_of_ones = held.tile([P, 1], F32, name="relu_of_ones")
+        nc.scalar.activation(relu_of_ones[:], ones[:, :1], mybir.ActivationFunctionType.Relu)
+
         identity = held.tile([P, P], BF16, name="identity")
         make_identity(nc, identity[:])
 
@@ -66,9 +69,12 @@ def tile_gather_matmul_kernel(tc, table, w, b, offs, out):
                         start=(c == 0),
                         stop=(c == K_BLOCKS - 1),
                     )
-            for a, queue in enumerate((nc.sync, nc.scalar)):
-                nc.vector.tensor_scalar(
-                    result[a][:, columns], banks[a][:], bias[:, a : a + 1], 0.0,
-                    op0=mybir.AluOpType.add, op1=mybir.AluOpType.max,
-                )
-                queue.dma_start(out_view[a][:, columns], result[a][:, columns])
+            nc.vector.tensor_scalar(
+                result[0][:, columns], banks[0][:], bias[:, 0:1], 0.0,
+                op0=mybir.AluOpType.add, op1=mybir.AluOpType.max,
+            )
+            nc.sync.dma_start(out_view[0][:, columns], result[0][:, columns])
+            nc.scalar.activation(
+                result[1][:, columns], banks[1][:], mybir.ActivationFunctionType.Relu, bias=bias[:, 1:2]
+            )
+            nc.scalar.dma_start(out_view[1][:, columns], result[1][:, columns])

@@ -33,7 +33,7 @@ def tile_gather_matmul_kernel(tc, table, w, b, offs, out):
         w_view = w.rearrange("e (p c) m -> e p c m", c=K_BLOCKS)
         weights = [held.tile([P, K_BLOCKS, M], BF16, name=f"weights{e}") for e in range(E)]
         for e in range(E):
-            nc.sync.dma_start(weights[e][:], w_view[e])
+            nc.scalar.dma_start(weights[e][:], w_view[e])
 
         ones = held.tile([P, P], BF16, name="ones")
         nc.vector.memset(ones[:], 1.0)

import concourse.mybir as mybir
from concourse.masks import make_identity

BF16, F32, U16 = mybir.dt.bfloat16, mybir.dt.float32, mybir.dt.uint16

P = 128
S, K, M, N, E = 256, 256, 256, 512, 4
Q = N // E
TOKEN_BLOCKS, K_BLOCKS, M_BLOCKS = S // P, K // P, M // P
Q_COLS = Q // 16
PSUM_BANKS = 8
WARM_MATMULS = 12

FLOPS = 2 * K * M * N


def tile_gather_matmul_kernel(tc, table, w, b, offs, out):
    nc = tc.nc
    with (
        tc.tile_pool(name="held", bufs=1) as held,
        tc.psum_pool(name="psum", bufs=PSUM_BANKS) as psum,
    ):
        token_rows = [held.tile([P, K], BF16, name=f"token_rows{t}") for t in range(TOKEN_BLOCKS)]
        nc.sync.dma_start(token_rows[0][:], table[0:P, :])
        nc.scalar.dma_start(token_rows[1][:], table[P : 2 * P, :])

        offsets = held.tile([P, N // 16], U16, name="offsets")
        nc.sync.dma_start(offsets[:], offs)

        bias = held.tile([P, M_BLOCKS], F32, name="bias")
        nc.scalar.dma_start(bias[:], b.rearrange("(p a) o -> p (a o)", a=M_BLOCKS))

        w_view = w.rearrange("e (p c) m -> e p c m", c=K_BLOCKS)
        weights = [held.tile([P, K_BLOCKS, M], BF16, name=f"weights{e}") for e in range(E)]
        for e in range(E):
            nc.scalar.dma_start(weights[e][:], w_view[e])

        ones = held.tile([P, P], BF16, name="ones")
        nc.vector.memset(ones[:], 1.0)
        unread = psum.tile([P, P], F32, name="unread", tag="bank")
        for repeat in range(WARM_MATMULS):
            nc.tensor.matmul(unread[:], ones[:], ones[:], start=True, stop=True)

        relu_of_ones = held.tile([P, 1], F32, name="relu_of_ones")
        nc.scalar.activation(relu_of_ones[:], ones[:, :1], mybir.ActivationFunctionType.Relu)

        identity = held.tile([P, P], BF16, name="identity")
        make_identity(nc, identity[:])

        features = [held.tile([P, S], BF16, name=f"features{c}") for c in range(K_BLOCKS)]
        for c in range(K_BLOCKS):
            for t in range(TOKEN_BLOCKS):
                flipped = psum.tile([P, P], BF16, name=f"flipped{c}{t}", tag="bank")
                nc.tensor.transpose(flipped[:], token_rows[t][:, c::K_BLOCKS], identity[:])
                nc.vector.tensor_copy(features[c][:, t * P : (t + 1) * P], flipped[:])

        out_view = out.rearrange("(p a) n -> a p n", a=M_BLOCKS)
        result = [held.tile([P, N], F32, name=f"result{a}") for a in range(M_BLOCKS)]
        for e in range(E):
            picked = offsets[:, e * Q_COLS : (e + 1) * Q_COLS]
            columns = slice(e * Q, (e + 1) * Q)
            banks = [psum.tile([P, Q], F32, name=f"sums{e}{a}", tag="bank") for a in range(M_BLOCKS)]
            for c in range(K_BLOCKS):
                for a in range(M_BLOCKS):
                    nc.tensor.matmul(
                        banks[a][:],
                        weights[e][:, c, a::M_BLOCKS],
                        features[c][:].indirect(picked),
                        start=(c == 0),
                        stop=(c == K_BLOCKS - 1),
                    )
            nc.vector.tensor_scalar(
                result[0][:, columns], banks[0][:], bias[:, 0:1], 0.0,
                op0=mybir.AluOpType.add, op1=mybir.AluOpType.max,
            )
            nc.sync.dma_start(out_view[0][:, columns], result[0][:, columns])
            nc.scalar.activation(
                result[1][:, columns], banks[1][:], mybir.ActivationFunctionType.Relu, bias=bias[:, 1:2]
            )
            nc.scalar.dma_start(out_view[1][:, columns], result[1][:, columns])
